import numpy as np
import ml_dtypes


def mxq(x, axis, fmt="e4m3"):
    dtype, down = {"e4m3": (ml_dtypes.float8_e4m3fn, 7), "e5m2": (ml_dtypes.float8_e5m2, 14)}[fmt]
    v = np.moveaxis(np.asarray(x, np.float32).astype(ml_dtypes.bfloat16).astype(np.float64), axis, -1)
    blocks = v.reshape(v.shape[:-1] + (-1, 32))
    amax = np.abs(blocks).max(-1, keepdims=True)
    byte = np.maximum(np.where(amax > 0, np.frexp(amax)[1] - 1 + 127, 0) - down, 1)
    scale = np.exp2(byte - 127.0)
    codes = (blocks / scale).astype(np.float32).astype(dtype).astype(np.float64)
    return np.moveaxis((codes * scale).reshape(v.shape), -1, axis)


WIDE = False


def mx_kscale(k):
    if not WIDE:
        return np.ones(k)
    levels = np.array([10, -10, 5, -5, 0])
    if k % 512:
        return np.exp2(np.random.permutation(np.resize(levels, k // 32))).repeat(32)
    a = np.empty((k // 512, 16))
    for p in range(k // 512):
        a[p, :8] = np.random.permutation(np.resize(levels, 8))
        for g in range(8):
            far = levels[np.abs(levels - a[p, g]) >= 10]
            a[p, g + 8] = far[np.random.randint(len(far))]
    return np.exp2(a.ravel()).repeat(32)


BF16 = ml_dtypes.bfloat16


def bf(x):
    return np.asarray(x, np.float32).astype(BF16)


def f64(x):
    return np.asarray(x).astype(np.float64)

def planes(Y):
    n, m = Y.shape
    b = f64(bf(Y)).reshape(n // 32, 32, m)
    amax = np.abs(b).max(1)
    byte = np.clip(np.where(amax > 0, np.frexp(amax)[1] - 1 + 127 - 7, 1), 1, 254)
    codes = (b * np.exp2(127.0 - byte)[:, None, :]).reshape(n, m).astype(np.float32).astype(ml_dtypes.float8_e4m3fn).view(np.uint8)
    words = codes.reshape(n // 512, 128, 4, m).transpose(0, 1, 3, 2)
    return np.ascontiguousarray(words), np.ascontiguousarray(byte.astype(np.uint8).reshape(n // 512, 16, m))


N, C, F = 1024, 512, 2048


def gelu_tanh(h):
    return 0.5 * h * (1.0 + np.tanh(np.sqrt(2.0 / np.pi) * (h + 0.044715 * (h * h * h))))


def setup_inputs():
    s = mx_kscale(C)
    t = mx_kscale(N)
    return {
        "x": bf(np.random.standard_normal((N, C)) * s[None, :]),
        "w1": bf(np.random.standard_normal((C, F)) / np.sqrt(C) / s[:, None]),
        "b1": bf(0.5 * np.random.standard_normal(F)),
        "r": bf((1.0 + 0.1 * np.random.standard_normal(N)) * t),
        "dy": bf(np.random.standard_normal((N, C)) / np.sqrt(N) / t[:, None]),
        "gamma": bf(1.0 + 0.1 * np.random.standard_normal(C)),
    }


def core(x, w1, b1, r, dy, gamma):
    h = (mxq(f64(x), 1, "e4m3") @ mxq(f64(w1), 0, "e4m3")) + f64(b1)[None, :]
    a = gelu_tanh(h)
    u = f64(r)[:, None] * a
    e = f64(dy) * f64(gamma)[None, :]
    return mxq(u, 0, "e4m3").T @ mxq(e, 0, "e4m3")


def reference(x, w1, b1, r, dy, gamma):
    R_out = core(x, w1, b1, r, dy, gamma)
    words, scales = planes(R_out.T)
    return R_out, words, scales

@@ -1,0 +1,381 @@
+from contextlib import ExitStack
+
+import concourse.mybir as mybir
+from concourse.masks import make_identity
+
+N, C, F = 1024, 512, 2048
+FLOPS = 4 * N * C * F
+
+F32 = mybir.dt.float32
+BF16 = mybir.dt.bfloat16
+I32 = mybir.dt.int32
+U32 = mybir.dt.uint32
+U8 = mybir.dt.uint8
+FP8X4 = mybir.dt.float8_e4m3fn_x4
+ACT = mybir.ActivationFunctionType
+MULT = mybir.AluOpType.mult
+
+P = 128
+G = 2
+TILES = F // P
+Q = 4
+
+
+def tile_convnextdroppathlayerscaleweightgrad_x1_kernel(tc, x, w1, b1, r, dy, gamma, out_0, out_1, out_2):
+    nc = tc.nc
+    with ExitStack() as ctx:
+        keep = ctx.enter_context(tc.tile_pool(name="keep", bufs=1))
+        work = ctx.enter_context(tc.tile_pool(name="work", bufs=3))
+        psum = ctx.enter_context(tc.psum_pool(name="psum", bufs=1))
+
+        ident = keep.tile([P, P], F32, name="ident")
+        ident_bf = keep.tile([P, P], BF16, name="ident_bf")
+        rows = keep.tile([P, P], BF16, name="rows")
+        cols = keep.tile([P, 20], F32, name="cols")
+        gcols = keep.tile([P, 4], BF16, name="gcols")
+        gam = keep.tile([P, C], BF16, name="gam")
+        r_sb = keep.tile([P, G, 4], BF16, name="r_sb")
+        warm = keep.tile([P, 1], F32, name="warm")
+        x_raw = [keep.tile([P, 4, C], BF16, name=f"x_raw{g}") for g in range(G)]
+        x_bf = [keep.tile([P, 4 * P, 4], BF16, name=f"x_bf{g}", align_bytes=64) for g in range(G)]
+        x_codes = keep.tile([P, G, 512], U32, name="x_codes", align_bytes=64)
+        x_scales = keep.tile([P, G, 512], U8, name="x_scales", align_bytes=64)
+        w_raw = [keep.tile([P, 4, Q * P], BF16, name=f"w_raw{q}") for q in range(TILES // Q)]
+        w_codes = keep.tile([P, F], U32, name="w_codes", align_bytes=64)
+        w_scales = keep.tile([P, F], U8, name="w_scales", align_bytes=64)
+        dy_raw = [keep.tile([P, 4, C], BF16, name=f"dy_raw{g}") for g in range(G)]
+        e_bf = [keep.tile([P, C, 4], BF16, name=f"e_bf{g}", align_bytes=64) for g in range(G)]
+        e_codes = keep.tile([P, G, C], U32, name="e_codes", align_bytes=64)
+        e_scales = keep.tile([P, G, C], U8, name="e_scales", align_bytes=64)
+        p_codes = keep.tile([P, F], U32, name="p_codes", align_bytes=64)
+        p_scales = keep.tile([P, F], U8, name="p_scales", align_bytes=64)
+
+        ctx.enter_context(tc.manual_schedule())
+        nc.gpsimd.memset(rows[:], 0.0)
+        nc.gpsimd.memset(warm[:], 0.0)
+        make_identity(nc, ident[:])
+
+        def load_x(g, t0, t1):
+            src = x[512 * g : 512 * g + 512, :].rearrange("(m t) k -> m t k", t=4)
+            nc.sync.dma_start(out=x_raw[g][:, t0:t1, :], in_=src[:, t0:t1, :])
+
+        def load_w(q, f0=0, n=Q):
+            c0 = q * Q * P + f0 * P
+            src = w1[:, c0 : c0 + n * P].rearrange("(p j) f -> p j f", j=4)
+            nc.sync.dma_start(out=w_raw[q][:, :, f0 * P : (f0 + n) * P], in_=src)
+
+        def load_dy(g):
+            src = dy[512 * g : 512 * g + 512, :].rearrange("(p j) c -> p j c", j=4)
+            nc.sync.dma_start(out=dy_raw[g][:], in_=src)
+
+        nc.scalar.dma_start(out=rows[0:16, :], in_=b1.rearrange("(i f) -> i f", f=P))
+        nc.scalar.dma_start(out=rows[16:20, :], in_=gamma.rearrange("(i f) -> i f", f=P))
+        nc.scalar.dma_start(out=r_sb[:], in_=r.rearrange("(g p t) -> p g t", g=G, t=4))
+        load_x(0, 0, 2)
+        load_x(0, 2, 4)
+        load_w(0, 0, 2)
+        load_x(1, 0, 4)
+        load_dy(0)
+        load_w(0, 2, 2)
+        load_dy(1)
+        load_w(1)
+        load_w(2)
+        load_w(3)
+
+        def x_transpose(g, half):
+            words = x_raw[g][:].rearrange("p t k -> p (t k)").bitcast(F32)
+            bank = psum.tile([P, 2, 2, P], F32, name="t_bank", tag="t", bufs=4)
+            for i in range(2):
+                t = 2 * half + i
+                for u in range(2):
+                    nc.tensor.transpose(bank[:, i, u, :], words[:, 256 * t + u : 256 * (t + 1) : 2], ident[:])
+            return bank
+
+        def x_exit(copy, g, half, bank):
+            dst = x_bf[g][:, 256 * half : 256 * half + 256, :].rearrange("p c j -> p (c j)").bitcast(F32)
+            copy(
+                out=dst.rearrange("p (t m u) -> p t m u", t=2, u=2),
+                in_=bank[:].rearrange("p t u m -> p t m u"),
+            )
+
+        def x_quant(g):
+            nc.vector.quantize_mx(
+                out=x_codes[:, g, :].bitcast(FP8X4),
+                scales=x_scales[:, g, :],
+                in_=x_bf[g][:].rearrange("p c j -> p (c j)"),
+            )
+
+        def w_group(copy, i, n):
+            q, f0 = divmod(i, Q)
+            grouped = work.tile([P, 2 * P, 4], BF16, name="w_bf", bufs=4, align_bytes=64)
+            copy(
+                out=grouped[:, : n * P, :],
+                in_=w_raw[q][:, :, f0 * P : (f0 + n) * P].rearrange("p j f -> p f j"),
+            )
+            return grouped
+
+        def w_quant(i, n, grouped):
+            cols_ = slice(i * P, (i + n) * P)
+            nc.vector.quantize_mx(
+                out=w_codes[:, cols_].bitcast(FP8X4),
+                scales=w_scales[:, cols_],
+                in_=grouped[:, : n * P, :].rearrange("p c j -> p (c j)"),
+            )
+
+        def e_mult(g, t0, t1):
+            nc.vector.tensor_tensor(
+                out=e_bf[g][:, t0 * P : t1 * P, :].rearrange("p (t m) j -> p t m j", m=P),
+                in0=dy_raw[g][:].rearrange("p j (m t) -> p t m j", t=4)[:, t0:t1],
+                in1=gam[:].rearrange("p (m t) -> p t m", t=4)[:, t0:t1].unsqueeze(3).to_broadcast([P, t1 - t0, P, 4]),
+                op=MULT,
+            )
+
+        def e_quant(g):
+            nc.vector.quantize_mx(
+                out=e_codes[:, g, :].bitcast(FP8X4),
+                scales=e_scales[:, g, :],
+                in_=e_bf[g][:].rearrange("p c j -> p (c j)"),
+            )
+
+        def stage1(i, g):
+            bank = psum.tile([P, 512], F32, name="h_bank", tag="h", bufs=2)
+            nc.tensor.matmul_mx(
+                out=bank[:],
+                lhsT=w_codes[:, i * P : (i + 1) * P].bitcast(FP8X4),
+                lhsT_scale=w_scales[:, i * P : (i + 1) * P],
+                rhs=x_codes[:, g, :].bitcast(FP8X4),
+                rhs_scale=x_scales[:, g, :],
+                start=True,
+                stop=True,
+            )
+            return bank
+
+        def gelu(i, g, bank):
+            a = work.tile([P, 512], F32, name="a_sb", bufs=6)
+            nc.scalar.activation(out=a[:], in_=bank[:], func=ACT.Gelu_apprx_tanh, bias=cols[:, i : i + 1])
+            return a
+
+        def turn(a):
+            bank = psum.tile([P, 4, P], F32, name="t_bank", tag="t", bufs=4)
+            for t in range(4):
+                nc.tensor.transpose(bank[:, t, :], a[:, t * P : (t + 1) * P], ident[:])
+            return bank
+
+        def u_mult(u, g, bank):
+            nc.vector.tensor_tensor(
+                out=u[:, g, :, :],
+                in0=bank[:].rearrange("p t f -> p f t"),
+                in1=r_sb[:, g, :].unsqueeze(1).to_broadcast([P, P, 4]),
+                op=MULT,
+            )
+
+        def u_quant(u):
+            codes = work.tile([P, G, P], U32, name="u_codes", bufs=8, align_bytes=64)
+            scales = work.tile([P, G, P], U8, name="u_scales", bufs=8, align_bytes=64)
+            nc.vector.quantize_mx(
+                out=codes[:].rearrange("p g f -> p (g f)").bitcast(FP8X4),
+                scales=scales[:].rearrange("p g f -> p (g f)"),
+                in_=u[:].rearrange("p g f t -> p (g f t)"),
+            )
+            return codes, scales
+
+        def stage2_r(u):
+            codes, scales = u
+            r_bank = psum.tile([P, C], F32, name="r_bank", tag="rp", bufs=2)
+            for g in range(G):
+                nc.tensor.matmul_mx(
+                    out=r_bank[:],
+                    lhsT=codes[:, g, :].bitcast(FP8X4),
+                    lhsT_scale=scales[:, g, :],
+                    rhs=e_codes[:, g, :].bitcast(FP8X4),
+                    rhs_scale=e_scales[:, g, :],
+                    start=(g == 0),
+                    stop=(g == G - 1),
+                )
+            return r_bank
+
+        def stage2_p(u):
+            codes, scales = u
+            p_bank = psum.tile([P, 4, P], F32, name="p_bank", tag="rp", bufs=2)
+            for t in range(4):
+                for g in range(G):
+                    nc.tensor.matmul_mx(
+                        out=p_bank[:, t, :],
+                        lhsT=e_codes[:, g, t * P : (t + 1) * P].bitcast(FP8X4),
+                        lhsT_scale=e_scales[:, g, t * P : (t + 1) * P],
+                        rhs=codes[:, g, :].bitcast(FP8X4),
+                        rhs_scale=scales[:, g, :],
+                        start=(g == 0),
+                        stop=(g == G - 1),
+                    )
+            return p_bank
+
+        def r_exit(copy, i, r_bank):
+            r_out = work.tile([P, P, 4], F32, name="r_out", bufs=4)
+            copy(out=r_out[:], in_=r_bank[:].rearrange("p (t m) -> p m t", t=4))
+            nc.sync.dma_start(out=out_0[i * P : (i + 1) * P, :], in_=r_out[:].rearrange("p m t -> p (m t)"))
+
+        def p_exit(copy, p_bank):
+            p_bf = work.tile([P, P, 4], BF16, name="p_bf", bufs=4, align_bytes=64)
+            copy(out=p_bf[:], in_=p_bank[:].rearrange("p t f -> p f t"))
+            return p_bf
+
+        def p_quant(i, p_bf):
+            nc.vector.quantize_mx(
+                out=p_codes[:, i * P : (i + 1) * P].bitcast(FP8X4),
+                scales=p_scales[:, i * P : (i + 1) * P],
+                in_=p_bf[:].rearrange("p f t -> p (f t)"),
+            )
+
+        def store_words(i0, i1):
+            nc.sync.dma_start(
+                out=out_1[0, :, i0 * P : i1 * P, :].rearrange("p m t -> p (m t)").bitcast(I32),
+                in_=p_codes[:, i0 * P : i1 * P].bitcast(I32),
+            )
+
+        def store_scales(i0, i1):
+            for quadrant in range(4):
+                nc.sync.dma_start(
+                    out=out_2[0, 4 * quadrant : 4 * quadrant + 4, i0 * P : i1 * P].bitcast(I32),
+                    in_=p_scales[32 * quadrant : 32 * quadrant + 4, i0 * P : i1 * P].bitcast(I32),
+                )
+
+
+        vcopy, scopy = nc.vector.tensor_copy, nc.scalar.copy
+        h, a, tb, u, uq, pb, wg = {}, {}, {}, {}, {}, {}, {}
+
+        def front(i, g):
+            h[i, g] = stage1(i, g)
+
+        def act(i, g):
+            a[i, g] = gelu(i, g, h[i, g])
+
+        def flip(i, g):
+            tb[i, g] = turn(a[i, g])
+
+        def mult(i, g):
+            if g == 0:
+                u[i] = work.tile([P, G, P, 4], BF16, name="u_bf", bufs=5, align_bytes=64)
+            u_mult(u[i], g, tb[i, g])
+
+        def uquant(i):
+            uq[i] = u_quant(u[i])
+
+        def wgroup(copy, i, n):
+            wg[i] = w_group(copy, i, n)
+
+        def wquant(i, n):
+            w_quant(i, n, wg[i])
+
+        def outp(copy, i):
+            pb[i] = p_exit(copy, stage2_p(uq[i]))
+
+        def outr(copy, i):
+            r_exit(copy, i, stage2_r(uq[i]))
+
+        def pquant(i):
+            p_quant(i, pb[i])
+            if i in (3, 7, 11):
+                store_words(i - 3, i + 1)
+            if i in (13, 15):
+                store_words(i - 1, i + 1)
+            if i == 11:
+                store_scales(0, 12)
+            if i == 15:
+                store_scales(12, 16)
+
+
+        def second(i, r_copy):
+            outp(scopy, i)
+            outr(r_copy, i)
+
+        def front2(i):
+            for g in range(G):
+                front(i, g)
+                act(i, g)
+
+        def flip2(i):
+            flip(i, 0)
+            flip(i, 1)
+
+        def mult2(i):
+            mult(i, 0)
+            mult(i, 1)
+
+        nc.scalar.activation(out=warm[:], in_=warm[:], func=ACT.Gelu_apprx_tanh)
+        nc.vector.tensor_copy(out=ident_bf[:], in_=ident[:])
+        x00 = x_transpose(0, 0)
+        x01 = x_transpose(0, 1)
+        cbank = psum.tile([P, P], BF16, name="c_bank", tag="rp", bufs=2)
+        nc.tensor.transpose(cbank[:], rows[:], ident_bf[:])
+        x_exit(scopy, 0, 1, x01)
+        nc.scalar.copy(out=cols[:], in_=cbank[:, 0:20])
+        nc.scalar.copy(out=gcols[:], in_=cbank[:, 16:20])
+        gbank = psum.tile([P, C], BF16, name="g_bank", tag="rp", bufs=2)
+        for j in range(4):
+            nc.tensor.transpose(gbank[:, j * P : (j + 1) * P], gcols[:, j : j + 1].to_broadcast([P, P]), ident_bf[:])
+        x_exit(vcopy, 0, 0, x00)
+        wgroup(scopy, 1, 1)
+        wgroup(vcopy, 0, 1)
+        nc.scalar.copy(out=gam[:], in_=gbank[:])
+        x10 = x_transpose(1, 0)
+        x11 = x_transpose(1, 1)
+        x_exit(scopy, 1, 0, x10)
+        x_exit(scopy, 1, 1, x11)
+        x_quant(0)
+        wquant(0, 1)
+        wquant(1, 1)
+        front(0, 0)
+        act(0, 0)
+        front(1, 0)
+        act(1, 0)
+        wgroup(scopy, 2, 2)
+        e_mult(0, 0, 2)
+        e_mult(0, 2, 4)
+        x_quant(1)
+        front(0, 1)
+        act(0, 1)
+        front(1, 1)
+        act(1, 1)
+        e_quant(0)
+        wquant(2, 2)
+        e_mult(1, 0, 2)
+        e_mult(1, 2, 4)
+        wgroup(vcopy, 4, 2)
+        e_quant(1)
+        wquant(4, 2)
+        flip2(0)
+        flip2(1)
+        front2(2)
+        front2(3)
+
+        for k in range(2, TILES // 2 + 3):
+            even, odd = 2 * k - 4, 2 * k - 3
+            if even < TILES:
+                mult2(even)
+            if 0 <= odd - 2 < TILES:
+                second(odd - 2, vcopy if odd - 2 == TILES - 1 else scopy)
+            for i in (2 * k - 7, 2 * k - 6):
+                if 0 <= i < TILES:
+                    pquant(i)
+            if even < TILES:
+                uquant(even)
+            if 2 * k + 2 < TILES:
+                wgroup(vcopy, 2 * k + 2, 2)
+            if 2 * k < TILES:
+                front2(2 * k)
+                second(even, scopy)
+            if odd < TILES:
+                mult2(odd)
+            if 2 * k < TILES:
+                front2(2 * k + 1)
+            if 2 * k + 2 < TILES:
+                wquant(2 * k + 2, 2)
+            if odd < TILES:
+                uquant(odd)
+            for i in (2 * k - 2, 2 * k - 1):
+                if i < TILES:
+                    flip2(i)
+            if 2 * k >= TILES and even < TILES:
+                second(even, scopy)
+        pquant(TILES - 1)

@@ -12,21 +12,23 @@ I32 = mybir.dt.int32
 U32 = mybir.dt.uint32
 U8 = mybir.dt.uint8
 FP8X4 = mybir.dt.float8_e4m3fn_x4
-ACT = mybir.ActivationFunctionType
+GELU = mybir.ActivationFunctionType.Gelu_apprx_tanh
 MULT = mybir.AluOpType.mult
 
 P = 128
-G = 2
+G = N // 512
 TILES = F // P
-Q = 4
+DIRECT = 12
 
 
 def tile_convnextdroppathlayerscaleweightgrad_x1_kernel(tc, x, w1, b1, r, dy, gamma, out_0, out_1, out_2):
     nc = tc.nc
+    vcopy, scopy = nc.vector.tensor_copy, nc.scalar.copy
     with ExitStack() as ctx:
         keep = ctx.enter_context(tc.tile_pool(name="keep", bufs=1))
         work = ctx.enter_context(tc.tile_pool(name="work", bufs=3))
         psum = ctx.enter_context(tc.psum_pool(name="psum", bufs=1))
+        ctx.enter_context(tc.manual_schedule())
 
         ident = keep.tile([P, P], F32, name="ident")
         ident_bf = keep.tile([P, P], BF16, name="ident_bf")
@@ -40,7 +42,7 @@ def tile_convnextdroppathlayerscaleweightgrad_x1_kernel(tc, x, w1, b1, r, dy, ga
         x_bf = [keep.tile([P, 4 * P, 4], BF16, name=f"x_bf{g}", align_bytes=64) for g in range(G)]
         x_codes = keep.tile([P, G, 512], U32, name="x_codes", align_bytes=64)
         x_scales = keep.tile([P, G, 512], U8, name="x_scales", align_bytes=64)
-        w_raw = [keep.tile([P, 4, Q * P], BF16, name=f"w_raw{q}") for q in range(TILES // Q)]
+        w_raw = keep.tile([P, 4, F], BF16, name="w_raw")
         w_codes = keep.tile([P, F], U32, name="w_codes", align_bytes=64)
         w_scales = keep.tile([P, F], U8, name="w_scales", align_bytes=64)
         dy_raw = [keep.tile([P, 4, C], BF16, name=f"dy_raw{g}") for g in range(G)]
@@ -50,45 +52,25 @@ def tile_convnextdroppathlayerscaleweightgrad_x1_kernel(tc, x, w1, b1, r, dy, ga
         p_codes = keep.tile([P, F], U32, name="p_codes", align_bytes=64)
         p_scales = keep.tile([P, F], U8, name="p_scales", align_bytes=64)
 
-        ctx.enter_context(tc.manual_schedule())
-        nc.gpsimd.memset(rows[:], 0.0)
-        nc.gpsimd.memset(warm[:], 0.0)
-        make_identity(nc, ident[:])
-
         def load_x(g, t0, t1):
             src = x[512 * g : 512 * g + 512, :].rearrange("(m t) k -> m t k", t=4)
             nc.sync.dma_start(out=x_raw[g][:, t0:t1, :], in_=src[:, t0:t1, :])
 
-        def load_w(q, f0=0, n=Q):
-            c0 = q * Q * P + f0 * P
-            src = w1[:, c0 : c0 + n * P].rearrange("(p j) f -> p j f", j=4)
-            nc.sync.dma_start(out=w_raw[q][:, :, f0 * P : (f0 + n) * P], in_=src)
+        def load_w(i0, i1):
+            c = slice(i0 * P, i1 * P)
+            nc.sync.dma_start(out=w_raw[:, :, c], in_=w1[:, c].rearrange("(p j) f -> p j f", j=4))
 
         def load_dy(g):
             src = dy[512 * g : 512 * g + 512, :].rearrange("(p j) c -> p j c", j=4)
             nc.sync.dma_start(out=dy_raw[g][:], in_=src)
 
-        nc.scalar.dma_start(out=rows[0:16, :], in_=b1.rearrange("(i f) -> i f", f=P))
-        nc.scalar.dma_start(out=rows[16:20, :], in_=gamma.rearrange("(i f) -> i f", f=P))
-        nc.scalar.dma_start(out=r_sb[:], in_=r.rearrange("(g p t) -> p g t", g=G, t=4))
-        load_x(0, 0, 2)
-        load_x(0, 2, 4)
-        load_w(0, 0, 2)
-        load_x(1, 0, 4)
-        load_dy(0)
-        load_w(0, 2, 2)
-        load_dy(1)
-        load_w(1)
-        load_w(2)
-        load_w(3)
-
         def x_transpose(g, half):
             words = x_raw[g][:].rearrange("p t k -> p (t k)").bitcast(F32)
-            bank = psum.tile([P, 2, 2, P], F32, name="t_bank", tag="t", bufs=4)
-            for i in range(2):
-                t = 2 * half + i
+            bank = psum.tile([P, 2, 2, P], F32, name="x_bank", tag="t", bufs=3)
+            for n in range(2):
+                t = 2 * half + n
                 for u in range(2):
-                    nc.tensor.transpose(bank[:, i, u, :], words[:, 256 * t + u : 256 * (t + 1) : 2], ident[:])
+                    nc.tensor.transpose(bank[:, n, u, :], words[:, 256 * t + u : 256 * (t + 1) : 2], ident[:])
             return bank
 
         def x_exit(copy, g, half, bank):
@@ -105,21 +87,23 @@ def tile_convnextdroppathlayerscaleweightgrad_x1_kernel(tc, x, w1, b1, r, dy, ga
                 in_=x_bf[g][:].rearrange("p c j -> p (c j)"),
             )
 
-        def w_group(copy, i, n):
-            q, f0 = divmod(i, Q)
-            grouped = work.tile([P, 2 * P, 4], BF16, name="w_bf", bufs=4, align_bytes=64)
-            copy(
-                out=grouped[:, : n * P, :],
-                in_=w_raw[q][:, :, f0 * P : (f0 + n) * P].rearrange("p j f -> p f j"),
-            )
-            return grouped
+        wg = {}
 
-        def w_quant(i, n, grouped):
-            cols_ = slice(i * P, (i + n) * P)
+        def w_group(copy, i, n):
+            wg[i] = work.tile([P, 2 * P, 4], BF16, name="w_bf", bufs=4, align_bytes=64)
+            src = w_raw[:, :, i * P : (i + n) * P]
+            dst = wg[i][:, : n * P, :]
+            copy(
+                out=dst.rearrange("p (c q) j -> p c j q", q=4),
+                in_=src.rearrange("p j (c q) -> p c j q", q=4),
+            )
+
+        def w_quant(i, n):
+            c = slice(i * P, (i + n) * P)
             nc.vector.quantize_mx(
-                out=w_codes[:, cols_].bitcast(FP8X4),
-                scales=w_scales[:, cols_],
-                in_=grouped[:, : n * P, :].rearrange("p c j -> p (c j)"),
+                out=w_codes[:, c].bitcast(FP8X4),
+                scales=w_scales[:, c],
+                in_=wg[i][:, : n * P, :].rearrange("p c j -> p (c j)"),
             )
 
         def e_mult(g, t0, t1):
@@ -137,54 +121,61 @@ def tile_convnextdroppathlayerscaleweightgrad_x1_kernel(tc, x, w1, b1, r, dy, ga
                 in_=e_bf[g][:].rearrange("p c j -> p (c j)"),
             )
 
+        a = {}
+
         def stage1(i, g):
             bank = psum.tile([P, 512], F32, name="h_bank", tag="h", bufs=2)
+            c = slice(i * P, (i + 1) * P)
             nc.tensor.matmul_mx(
                 out=bank[:],
-                lhsT=w_codes[:, i * P : (i + 1) * P].bitcast(FP8X4),
-                lhsT_scale=w_scales[:, i * P : (i + 1) * P],
+                lhsT=w_codes[:, c].bitcast(FP8X4),
+                lhsT_scale=w_scales[:, c],
                 rhs=x_codes[:, g, :].bitcast(FP8X4),
                 rhs_scale=x_scales[:, g, :],
                 start=True,
                 stop=True,
             )
-            return bank
+            a[i, g] = work.tile([P, 512], F32, name="a_sb", bufs=8)
+            nc.scalar.activation(out=a[i, g][:], in_=bank[:], func=GELU, bias=cols[:, i : i + 1])
 
-        def gelu(i, g, bank):
-            a = work.tile([P, 512], F32, name="a_sb", bufs=6)
-            nc.scalar.activation(out=a[:], in_=bank[:], func=ACT.Gelu_apprx_tanh, bias=cols[:, i : i + 1])
-            return a
+        turned = {}
+        u = {}
 
-        def turn(a):
-            bank = psum.tile([P, 4, P], F32, name="t_bank", tag="t", bufs=4)
+        def turn(i, g):
+            turned[i, g] = psum.tile([P, 4, P], F32, name="t_bank", tag="t", bufs=3)
             for t in range(4):
-                nc.tensor.transpose(bank[:, t, :], a[:, t * P : (t + 1) * P], ident[:])
-            return bank
+                nc.tensor.transpose(turned[i, g][:, t, :], a[i, g][:, t * P : (t + 1) * P], ident[:])
 
-        def u_mult(u, g, bank):
+        def u_mult(i, g):
+            if g == 0:
+                u[i] = work.tile([P, G, P, 4], BF16, name="u_bf", bufs=4, align_bytes=64)
             nc.vector.tensor_tensor(
-                out=u[:, g, :, :],
-                in0=bank[:].rearrange("p t f -> p f t"),
+                out=u[i][:, g, :, :],
+                in0=turned[i, g][:].rearrange("p t f -> p f t"),
                 in1=r_sb[:, g, :].unsqueeze(1).to_broadcast([P, P, 4]),
                 op=MULT,
             )
 
-        def u_quant(u):
+        uq = {}
+
+        def u_quant(i):
             codes = work.tile([P, G, P], U32, name="u_codes", bufs=8, align_bytes=64)
             scales = work.tile([P, G, P], U8, name="u_scales", bufs=8, align_bytes=64)
             nc.vector.quantize_mx(
                 out=codes[:].rearrange("p g f -> p (g f)").bitcast(FP8X4),
                 scales=scales[:].rearrange("p g f -> p (g f)"),
-                in_=u[:].rearrange("p g f t -> p (g f t)"),
+                in_=u[i][:].rearrange("p g f t -> p (g f t)"),
             )
-            return codes, scales
+            uq[i] = codes, scales
 
-        def stage2_r(u):
-            codes, scales = u
-            r_bank = psum.tile([P, C], F32, name="r_bank", tag="rp", bufs=2)
+        r_out = {}
+
+        def stage2_r(i, copy):
+            codes, scales = uq[i]
+            bank = psum.tile([P, C], F32, name="r_bank", tag="r", bufs=2)
             for g in range(G):
                 nc.tensor.matmul_mx(
-                    out=r_bank[:],
+                    out=bank[:],
                     lhsT=codes[:, g, :].bitcast(FP8X4),
                     lhsT_scale=scales[:, g, :],
                     rhs=e_codes[:, g, :].bitcast(FP8X4),
@@ -192,39 +183,37 @@ def tile_convnextdroppathlayerscaleweightgrad_x1_kernel(tc, x, w1, b1, r, dy, ga
                     start=(g == 0),
                     stop=(g == G - 1),
                 )
-            return r_bank
+            j, n = divmod(i, 2)
+            if n == 0:
+                r_out[j] = work.tile([P, 2, C], F32, name="r_out", bufs=4)
+            dst = r_out[j][:, n, :]
+            copy(
+                out=dst.rearrange("p (m t) -> p m t", t=4),
+                in_=bank[:].rearrange("p (t m) -> p m t", t=4),
+            )
+            nc.sync.dma_start(out=out_0[i * P : (i + 1) * P, :], in_=dst)
 
-        def stage2_p(u):
-            codes, scales = u
-            p_bank = psum.tile([P, 4, P], F32, name="p_bank", tag="rp", bufs=2)
-            for t in range(4):
-                for g in range(G):
-                    nc.tensor.matmul_mx(
-                        out=p_bank[:, t, :],
-                        lhsT=e_codes[:, g, t * P : (t + 1) * P].bitcast(FP8X4),
-                        lhsT_scale=e_scales[:, g, t * P : (t + 1) * P],
-                        rhs=codes[:, g, :].bitcast(FP8X4),
-                        rhs_scale=scales[:, g, :],
-                        start=(g == 0),
-                        stop=(g == G - 1),
-                    )
-            return p_bank
+        r_bf = {}
+        p_turned = {}
+        p_bf = {}
 
-        def r_exit(copy, i, r_bank):
-            r_out = work.tile([P, P, 4], F32, name="r_out", bufs=4)
-            copy(out=r_out[:], in_=r_bank[:].rearrange("p (t m) -> p m t", t=4))
-            nc.sync.dma_start(out=out_0[i * P : (i + 1) * P, :], in_=r_out[:].rearrange("p m t -> p (m t)"))
+        def p_cast(j):
+            r_bf[j] = work.tile([P, 2, C], BF16, name="r_bf", bufs=2)
+            vcopy(out=r_bf[j][:], in_=r_out[j][:])
 
-        def p_exit(copy, p_bank):
-            p_bf = work.tile([P, P, 4], BF16, name="p_bf", bufs=4, align_bytes=64)
-            copy(out=p_bf[:], in_=p_bank[:].rearrange("p t f -> p f t"))
-            return p_bf
+        def p_turn(j):
+            words = r_bf[j][:].rearrange("p n c -> p (n c)").bitcast(F32)
+            p_turned[j] = psum.tile([P, 2, 2, P], F32, name="p_bank", tag="p", bufs=1)
+            for n in range(2):
+                for v in range(2):
+                    nc.tensor.transpose(p_turned[j][:, n, v, :], words[:, 256 * n + v : 256 * (n + 1) : 2], ident[:])
 
-        def p_quant(i, p_bf):
-            nc.vector.quantize_mx(
-                out=p_codes[:, i * P : (i + 1) * P].bitcast(FP8X4),
-                scales=p_scales[:, i * P : (i + 1) * P],
-                in_=p_bf[:].rearrange("p f t -> p (f t)"),
+        def p_exit(j, copy):
+            p_bf[j] = work.tile([P, 2, P, 4], BF16, name="p_bf", bufs=3, align_bytes=64)
+            dst = p_bf[j][:].rearrange("p n f c -> p (n f c)").bitcast(F32)
+            copy(
+                out=dst.rearrange("p (n f v) -> p n f v", n=2, v=2),
+                in_=p_turned[j][:].rearrange("p n v f -> p n f v"),
             )
 
         def store_words(i0, i1):
@@ -240,142 +229,155 @@ def tile_convnextdroppathlayerscaleweightgrad_x1_kernel(tc, x, w1, b1, r, dy, ga
                     in_=p_scales[32 * quadrant : 32 * quadrant + 4, i0 * P : i1 * P].bitcast(I32),
                 )
 
+        def p_quant(j):
+            c = slice(2 * j * P, (2 * j + 2) * P)
+            nc.vector.quantize_mx(
+                out=p_codes[:, c].bitcast(FP8X4),
+                scales=p_scales[:, c],
+                in_=p_bf[j][:].rearrange("p n f c -> p (n f c)"),
+            )
+            if j % 2 == 1:
+                store_words(2 * j - 2, 2 * j + 2)
+            if 2 * j + 2 == DIRECT:
+                store_scales(0, DIRECT)
 
-        vcopy, scopy = nc.vector.tensor_copy, nc.scalar.copy
-        h, a, tb, u, uq, pb, wg = {}, {}, {}, {}, {}, {}, {}
+        d_bf = {}
 
-        def front(i, g):
-            h[i, g] = stage1(i, g)
+        def stage2_p(i, copy):
+            codes, scales = uq[i]
+            bank = psum.tile([P, 4, P], F32, name="d_bank", tag="h", bufs=2)
+            for t in range(4):
+                for g in range(G):
+                    nc.tensor.matmul_mx(
+                        out=bank[:, t, :],
+                        lhsT=e_codes[:, g, t * P : (t + 1) * P].bitcast(FP8X4),
+                        lhsT_scale=e_scales[:, g, t * P : (t + 1) * P],
+                        rhs=codes[:, g, :].bitcast(FP8X4),
+                        rhs_scale=scales[:, g, :],
+                        start=(g == 0),
+                        stop=(g == G - 1),
+                    )
+            d_bf[i] = work.tile([P, P, 4], BF16, name="d_bf", bufs=4, align_bytes=64)
+            copy(out=d_bf[i][:], in_=bank[:].rearrange("p t f -> p f t"))
 
-        def act(i, g):
-            a[i, g] = gelu(i, g, h[i, g])
-
-        def flip(i, g):
-            tb[i, g] = turn(a[i, g])
-
-        def mult(i, g):
-            if g == 0:
-                u[i] = work.tile([P, G, P, 4], BF16, name="u_bf", bufs=5, align_bytes=64)
-            u_mult(u[i], g, tb[i, g])
-
-        def uquant(i):
-            uq[i] = u_quant(u[i])
-
-        def wgroup(copy, i, n):
-            wg[i] = w_group(copy, i, n)
-
-        def wquant(i, n):
-            w_quant(i, n, wg[i])
-
-        def outp(copy, i):
-            pb[i] = p_exit(copy, stage2_p(uq[i]))
-
-        def outr(copy, i):
-            r_exit(copy, i, stage2_r(uq[i]))
-
-        def pquant(i):
-            p_quant(i, pb[i])
-            if i in (3, 7, 11):
-                store_words(i - 3, i + 1)
-            if i in (13, 15):
+        def d_quant(i):
+            c = slice(i * P, (i + 1) * P)
+            nc.vector.quantize_mx(
+                out=p_codes[:, c].bitcast(FP8X4),
+                scales=p_scales[:, c],
+                in_=d_bf[i][:].rearrange("p f t -> p (f t)"),
+            )
+            if i % 2 == 1:
                 store_words(i - 1, i + 1)
-            if i == 11:
-                store_scales(0, 12)
-            if i == 15:
-                store_scales(12, 16)
+            if i == TILES - 1:
+                store_scales(DIRECT, TILES)
 
+        nc.gpsimd.memset(rows[:], 0.0)
+        nc.gpsimd.memset(warm[:], 0.0)
+        make_identity(nc, ident[:])
+        nc.scalar.dma_start(out=rows[0:16, :], in_=b1.rearrange("(i f) -> i f", f=P))
+        nc.scalar.dma_start(out=rows[16:20, :], in_=gamma.rearrange("(i f) -> i f", f=P))
+        nc.scalar.dma_start(out=r_sb[:], in_=r.rearrange("(g p t) -> p g t", g=G, t=4))
+        load_x(0, 0, 2)
+        load_x(0, 2, 4)
+        load_w(0, 2)
+        load_x(1, 0, 4)
+        load_w(2, 4)
+        load_dy(0)
+        load_dy(1)
+        load_w(4, 8)
+        load_w(8, 12)
+        load_w(12, 16)
 
-        def second(i, r_copy):
-            outp(scopy, i)
-            outr(r_copy, i)
-
-        def front2(i):
-            for g in range(G):
-                front(i, g)
-                act(i, g)
-
-        def flip2(i):
-            flip(i, 0)
-            flip(i, 1)
-
-        def mult2(i):
-            mult(i, 0)
-            mult(i, 1)
-
-        nc.scalar.activation(out=warm[:], in_=warm[:], func=ACT.Gelu_apprx_tanh)
-        nc.vector.tensor_copy(out=ident_bf[:], in_=ident[:])
+        nc.scalar.activation(out=warm[:], in_=warm[:], func=GELU)
+        vcopy(out=ident_bf[:], in_=ident[:])
         x00 = x_transpose(0, 0)
         x01 = x_transpose(0, 1)
-        cbank = psum.tile([P, P], BF16, name="c_bank", tag="rp", bufs=2)
-        nc.tensor.transpose(cbank[:], rows[:], ident_bf[:])
-        x_exit(scopy, 0, 1, x01)
-        nc.scalar.copy(out=cols[:], in_=cbank[:, 0:20])
-        nc.scalar.copy(out=gcols[:], in_=cbank[:, 16:20])
-        gbank = psum.tile([P, C], BF16, name="g_bank", tag="rp", bufs=2)
-        for j in range(4):
-            nc.tensor.transpose(gbank[:, j * P : (j + 1) * P], gcols[:, j : j + 1].to_broadcast([P, P]), ident_bf[:])
-        x_exit(vcopy, 0, 0, x00)
-        wgroup(scopy, 1, 1)
-        wgroup(vcopy, 0, 1)
-        nc.scalar.copy(out=gam[:], in_=gbank[:])
+        c_bank = psum.tile([P, P], BF16, name="c_bank", tag="r", bufs=2)
+        nc.tensor.transpose(c_bank[:], rows[:], ident_bf[:])
+        x_exit(scopy, 0, 0, x00)
+        x_exit(vcopy, 0, 1, x01)
+        scopy(out=cols[:], in_=c_bank[:, 0:20])
+        scopy(out=gcols[:], in_=c_bank[:, 16:20])
+        w_group(vcopy, 0, 1)
+        w_group(scopy, 1, 1)
+        g_bank = psum.tile([P, C], BF16, name="g_bank", tag="r", bufs=2)
+        for q in range(4):
+            nc.tensor.transpose(g_bank[:, q * P : (q + 1) * P], gcols[:, q : q + 1].to_broadcast([P, P]), ident_bf[:])
+        scopy(out=gam[:], in_=g_bank[:])
+        x_quant(0)
+        w_quant(0, 1)
+        w_quant(1, 1)
         x10 = x_transpose(1, 0)
         x11 = x_transpose(1, 1)
         x_exit(scopy, 1, 0, x10)
         x_exit(scopy, 1, 1, x11)
-        x_quant(0)
-        wquant(0, 1)
-        wquant(1, 1)
-        front(0, 0)
-        act(0, 0)
-        front(1, 0)
-        act(1, 0)
-        wgroup(scopy, 2, 2)
-        e_mult(0, 0, 2)
-        e_mult(0, 2, 4)
+        stage1(0, 0)
+        stage1(1, 0)
+        w_group(scopy, 2, 2)
         x_quant(1)
-        front(0, 1)
-        act(0, 1)
-        front(1, 1)
-        act(1, 1)
+        stage1(0, 1)
+        stage1(1, 1)
+        w_group(scopy, 4, 2)
+        for q in range(2):
+            e_mult(0, 2 * q, 2 * q + 2)
+        w_quant(2, 2)
+        for q in range(2):
+            e_mult(1, 2 * q, 2 * q + 2)
         e_quant(0)
-        wquant(2, 2)
-        e_mult(1, 0, 2)
-        e_mult(1, 2, 4)
-        wgroup(vcopy, 4, 2)
         e_quant(1)
-        wquant(4, 2)
-        flip2(0)
-        flip2(1)
-        front2(2)
-        front2(3)
+        w_quant(4, 2)
 
-        for k in range(2, TILES // 2 + 3):
-            even, odd = 2 * k - 4, 2 * k - 3
-            if even < TILES:
-                mult2(even)
-            if 0 <= odd - 2 < TILES:
-                second(odd - 2, vcopy if odd - 2 == TILES - 1 else scopy)
-            for i in (2 * k - 7, 2 * k - 6):
-                if 0 <= i < TILES:
-                    pquant(i)
-            if even < TILES:
-                uquant(even)
-            if 2 * k + 2 < TILES:
-                wgroup(vcopy, 2 * k + 2, 2)
-            if 2 * k < TILES:
-                front2(2 * k)
-                second(even, scopy)
-            if odd < TILES:
-                mult2(odd)
-            if 2 * k < TILES:
-                front2(2 * k + 1)
-            if 2 * k + 2 < TILES:
-                wquant(2 * k + 2, 2)
-            if odd < TILES:
-                uquant(odd)
-            for i in (2 * k - 2, 2 * k - 1):
-                if i < TILES:
-                    flip2(i)
-            if 2 * k >= TILES and even < TILES:
-                second(even, scopy)
-        pquant(TILES - 1)
+        for k in range(1, TILES // 2 + 2):
+            lead, mid = 2 * k, 2 * k - 2
+            if lead < TILES:
+                stage1(lead, 0)
+                stage1(lead, 1)
+            for i in (2 * k - 5, 2 * k - 4):
+                if 0 <= i:
+                    if i >= DIRECT:
+                        stage2_p(i, scopy)
+                    stage2_r(i, scopy)
+            if lead < TILES:
+                stage1(lead + 1, 0)
+                stage1(lead + 1, 1)
+            pair = k - 3
+            paired = 0 <= 2 * pair < DIRECT
+            if k == 1:
+                w_group(scopy, 6, 2)
+            if paired:
+                p_cast(pair)
+            if mid < TILES:
+                turn(mid, 0)
+                turn(mid, 1)
+                turn(mid + 1, 0)
+                u_mult(mid, 0)
+            if paired:
+                p_turn(pair)
+            if mid < TILES:
+                turn(mid + 1, 1)
+                u_mult(mid, 1)
+            if 0 <= mid - 1 < TILES:
+                u_quant(mid - 1)
+            if paired:
+                p_exit(pair, scopy)
+            if pair >= 1 and 2 * pair - 2 < DIRECT:
+                p_quant(pair - 1)
+            for i in (2 * k - 5, 2 * k - 4):
+                if DIRECT <= i < TILES - 1:
+                    d_quant(i)
+            if mid < TILES:
+                u_quant(mid)
+            if k >= 2 and 2 * k + 4 < TILES:
+                w_group(vcopy, 2 * k + 4, 2)
+            if mid < TILES:
+                u_mult(mid + 1, 0)
+                u_mult(mid + 1, 1)
+            if k == 1:
+                w_quant(6, 2)
+            if k >= 2 and 2 * k + 4 < TILES:
+                w_quant(2 * k + 4, 2)
+        i = TILES - 1
+        stage2_p(i, scopy)
+        stage2_r(i, vcopy)
+        d_quant(i)

@@ -18,6 +18,7 @@ MULT = mybir.AluOpType.mult
 P = 128
 G = N // 512
 TILES = F // P
+W_LOADS = ((0, 2), (2, 4), (4, 8), (8, 12), (12, 16))
 DIRECT = 12
 
 
@@ -42,7 +43,11 @@ def tile_convnextdroppathlayerscaleweightgrad_x1_kernel(tc, x, w1, b1, r, dy, ga
         x_bf = [keep.tile([P, 4 * P, 4], BF16, name=f"x_bf{g}", align_bytes=64) for g in range(G)]
         x_codes = keep.tile([P, G, 512], U32, name="x_codes", align_bytes=64)
         x_scales = keep.tile([P, G, 512], U8, name="x_scales", align_bytes=64)
-        w_raw = keep.tile([P, 4, F], BF16, name="w_raw")
+        w_raw = {}
+        for i0, i1 in W_LOADS:
+            raw = keep.tile([P, 4, (i1 - i0) * P], BF16, name=f"w_raw{i0}")
+            for i in range(i0, i1):
+                w_raw[i] = raw, i - i0
         w_codes = keep.tile([P, F], U32, name="w_codes", align_bytes=64)
         w_scales = keep.tile([P, F], U8, name="w_scales", align_bytes=64)
         dy_raw = [keep.tile([P, 4, C], BF16, name=f"dy_raw{g}") for g in range(G)]
@@ -58,7 +63,7 @@ def tile_convnextdroppathlayerscaleweightgrad_x1_kernel(tc, x, w1, b1, r, dy, ga
 
         def load_w(i0, i1):
             c = slice(i0 * P, i1 * P)
-            nc.sync.dma_start(out=w_raw[:, :, c], in_=w1[:, c].rearrange("(p j) f -> p j f", j=4))
+            nc.sync.dma_start(out=w_raw[i0][0][:], in_=w1[:, c].rearrange("(p j) f -> p j f", j=4))
 
         def load_dy(g):
             src = dy[512 * g : 512 * g + 512, :].rearrange("(p j) c -> p j c", j=4)
@@ -91,7 +96,8 @@ def tile_convnextdroppathlayerscaleweightgrad_x1_kernel(tc, x, w1, b1, r, dy, ga
 
         def w_group(copy, i, n):
             wg[i] = work.tile([P, 2 * P, 4], BF16, name="w_bf", bufs=4, align_bytes=64)
-            src = w_raw[:, :, i * P : (i + n) * P]
+            raw, at = w_raw[i]
+            src = raw[:, :, at * P : (at + n) * P]
             dst = wg[i][:, : n * P, :]
             copy(
                 out=dst.rearrange("p (c q) j -> p c j q", q=4),
@@ -224,7 +230,8 @@ def tile_convnextdroppathlayerscaleweightgrad_x1_kernel(tc, x, w1, b1, r, dy, ga
 
         def store_scales(i0, i1):
             for quadrant in range(4):
-                nc.sync.dma_start(
+                queue = nc.scalar if i1 == TILES and quadrant % 2 else nc.sync
+                queue.dma_start(
                     out=out_2[0, 4 * quadrant : 4 * quadrant + 4, i0 * P : i1 * P].bitcast(I32),
                     in_=p_scales[32 * quadrant : 32 * quadrant + 4, i0 * P : i1 * P].bitcast(I32),
                 )
@@ -238,6 +245,8 @@ def tile_convnextdroppathlayerscaleweightgrad_x1_kernel(tc, x, w1, b1, r, dy, ga
             )
             if j % 2 == 1:
                 store_words(2 * j - 2, 2 * j + 2)
+            elif 2 * j + 2 == DIRECT:
+                store_words(2 * j, 2 * j + 2)
             if 2 * j + 2 == DIRECT:
                 store_scales(0, DIRECT)
 
@@ -295,18 +304,18 @@ def tile_convnextdroppathlayerscaleweightgrad_x1_kernel(tc, x, w1, b1, r, dy, ga
         x01 = x_transpose(0, 1)
         c_bank = psum.tile([P, P], BF16, name="c_bank", tag="r", bufs=2)
         nc.tensor.transpose(c_bank[:], rows[:], ident_bf[:])
-        x_exit(scopy, 0, 0, x00)
-        x_exit(vcopy, 0, 1, x01)
+        w_group(vcopy, 0, 1)
+        x_exit(vcopy, 0, 0, x00)
+        x_exit(scopy, 0, 1, x01)
         scopy(out=cols[:], in_=c_bank[:, 0:20])
         scopy(out=gcols[:], in_=c_bank[:, 16:20])
-        w_group(vcopy, 0, 1)
         w_group(scopy, 1, 1)
         g_bank = psum.tile([P, C], BF16, name="g_bank", tag="r", bufs=2)
         for q in range(4):
             nc.tensor.transpose(g_bank[:, q * P : (q + 1) * P], gcols[:, q : q + 1].to_broadcast([P, P]), ident_bf[:])
         scopy(out=gam[:], in_=g_bank[:])
-        x_quant(0)
         w_quant(0, 1)
+        x_quant(0)
         w_quant(1, 1)
         x10 = x_transpose(1, 0)
         x11 = x_transpose(1, 1)
@@ -314,69 +323,68 @@ def tile_convnextdroppathlayerscaleweightgrad_x1_kernel(tc, x, w1, b1, r, dy, ga
         x_exit(scopy, 1, 1, x11)
         stage1(0, 0)
         stage1(1, 0)
-        w_group(scopy, 2, 2)
+        w_group(vcopy, 2, 2)
         x_quant(1)
         stage1(0, 1)
         stage1(1, 1)
-        w_group(scopy, 4, 2)
-        for q in range(2):
-            e_mult(0, 2 * q, 2 * q + 2)
+        e_mult(0, 0, 4)
         w_quant(2, 2)
-        for q in range(2):
-            e_mult(1, 2 * q, 2 * q + 2)
+        w_group(scopy, 4, 2)
         e_quant(0)
-        e_quant(1)
+        e_mult(1, 0, 4)
         w_quant(4, 2)
 
         for k in range(1, TILES // 2 + 2):
-            lead, mid = 2 * k, 2 * k - 2
-            if lead < TILES:
-                stage1(lead, 0)
-                stage1(lead, 1)
-            for i in (2 * k - 5, 2 * k - 4):
-                if 0 <= i:
+            lead, even, odd = 2 * k, 2 * k - 2, 2 * k - 1
+            ahead = [i for i in (2 * k - 5, 2 * k - 4) if i >= 0]
+            pair = k - 3
+            paired = 0 <= 2 * pair < DIRECT
+            for n in range(2):
+                if lead < TILES:
+                    stage1(lead, n)
+                for i in ahead[n : n + 1] if len(ahead) == 2 else ahead[n - 1 : n]:
                     if i >= DIRECT:
                         stage2_p(i, scopy)
                     stage2_r(i, scopy)
-            if lead < TILES:
-                stage1(lead + 1, 0)
-                stage1(lead + 1, 1)
-            pair = k - 3
-            paired = 0 <= 2 * pair < DIRECT
             if k == 1:
                 w_group(scopy, 6, 2)
+            if lead < TILES:
+                stage1(lead + 1, 0)
             if paired:
                 p_cast(pair)
-            if mid < TILES:
-                turn(mid, 0)
-                turn(mid, 1)
-                turn(mid + 1, 0)
-                u_mult(mid, 0)
+            if even < TILES:
+                turn(even, 0)
+                turn(even, 1)
+            if lead < TILES:
+                stage1(lead + 1, 1)
             if paired:
                 p_turn(pair)
-            if mid < TILES:
-                turn(mid + 1, 1)
-                u_mult(mid, 1)
-            if 0 <= mid - 1 < TILES:
-                u_quant(mid - 1)
-            if paired:
                 p_exit(pair, scopy)
-            if pair >= 1 and 2 * pair - 2 < DIRECT:
-                p_quant(pair - 1)
-            for i in (2 * k - 5, 2 * k - 4):
-                if DIRECT <= i < TILES - 1:
-                    d_quant(i)
-            if mid < TILES:
-                u_quant(mid)
-            if k >= 2 and 2 * k + 4 < TILES:
-                w_group(vcopy, 2 * k + 4, 2)
-            if mid < TILES:
-                u_mult(mid + 1, 0)
-                u_mult(mid + 1, 1)
+            if even < TILES:
+                u_mult(even, 0)
+                u_mult(even, 1)
+            if k == 1:
+                e_quant(1)
+            elif 2 * k + 4 < TILES:
+                w_quant(2 * k + 4, 2)
+            if even < TILES:
+                u_quant(even)
+                turn(odd, 0)
+            if even < TILES:
+                turn(odd, 1)
+                u_mult(odd, 0)
+                u_mult(odd, 1)
             if k == 1:
                 w_quant(6, 2)
-            if k >= 2 and 2 * k + 4 < TILES:
-                w_quant(2 * k + 4, 2)
+            if 2 * k + 6 < TILES:
+                w_group(vcopy, 2 * k + 6, 2)
+            if paired:
+                p_quant(pair)
+            if even < TILES:
+                u_quant(odd)
+            for i in ahead:
+                if i >= DIRECT:
+                    d_quant(i)
         i = TILES - 1
         stage2_p(i, scopy)
         stage2_r(i, vcopy)

@@ -19,6 +19,9 @@ P = 128
 G = N // 512
 TILES = F // P
 W_LOADS = ((0, 2), (2, 4), (4, 8), (8, 12), (12, 16))
+S_HALVES = {2: 12, 3: 13}
+V_GROUPS = {1: 8, 2: 10, 4: 14}
+QUANTS = {2: 8, 3: 10, 4: 12, 5: 14}
 DIRECT = 12
 
 
@@ -95,10 +98,12 @@ def tile_convnextdroppathlayerscaleweightgrad_x1_kernel(tc, x, w1, b1, r, dy, ga
         wg = {}
 
         def w_group(copy, i, n):
-            wg[i] = work.tile([P, 2 * P, 4], BF16, name="w_bf", bufs=4, align_bytes=64)
             raw, at = w_raw[i]
+            first = i - i % 2
+            if i == first:
+                wg[i] = work.tile([P, 2 * P, 4], BF16, name="w_bf", bufs=5, align_bytes=64)
             src = raw[:, :, at * P : (at + n) * P]
-            dst = wg[i][:, : n * P, :]
+            dst = wg[first][:, (i - first) * P : (i - first + n) * P, :]
             copy(
                 out=dst.rearrange("p (c q) j -> p c j q", q=4),
                 in_=src.rearrange("p j (c q) -> p c j q", q=4),
@@ -130,7 +135,7 @@ def tile_convnextdroppathlayerscaleweightgrad_x1_kernel(tc, x, w1, b1, r, dy, ga
         a = {}
 
         def stage1(i, g):
-            bank = psum.tile([P, 512], F32, name="h_bank", tag="h", bufs=2)
+            bank = psum.tile([P, 512], F32, name="h_bank", tag="h", bufs=3)
             c = slice(i * P, (i + 1) * P)
             nc.tensor.matmul_mx(
                 out=bank[:],
@@ -204,15 +209,18 @@ def tile_convnextdroppathlayerscaleweightgrad_x1_kernel(tc, x, w1, b1, r, dy, ga
         p_bf = {}
 
         def p_cast(j):
-            r_bf[j] = work.tile([P, 2, C], BF16, name="r_bf", bufs=2)
-            vcopy(out=r_bf[j][:], in_=r_out[j][:])
+            r_bf[j] = work.tile([P, 2, 2, P, 2], BF16, name="r_bf", bufs=2)
+            vcopy(
+                out=r_bf[j][:].rearrange("p v n m c -> p v (n m) c"),
+                in_=r_out[j][:].rearrange("p n (m v c) -> p v (n m) c", v=2, c=2),
+            )
 
         def p_turn(j):
-            words = r_bf[j][:].rearrange("p n c -> p (n c)").bitcast(F32)
-            p_turned[j] = psum.tile([P, 2, 2, P], F32, name="p_bank", tag="p", bufs=1)
+            words = r_bf[j][:].rearrange("p v n m c -> p (v n m c)").bitcast(F32)
+            p_turned[j] = psum.tile([P, 2, 2, P], F32, name="p_bank", tag="r", bufs=2)
             for n in range(2):
                 for v in range(2):
-                    nc.tensor.transpose(p_turned[j][:, n, v, :], words[:, 256 * n + v : 256 * (n + 1) : 2], ident[:])
+                    nc.tensor.transpose(p_turned[j][:, n, v, :], words[:, 128 * (2 * v + n) : 128 * (2 * v + n + 1)], ident[:])
 
         def p_exit(j, copy):
             p_bf[j] = work.tile([P, 2, P, 4], BF16, name="p_bf", bufs=3, align_bytes=64)
@@ -254,7 +262,7 @@ def tile_convnextdroppathlayerscaleweightgrad_x1_kernel(tc, x, w1, b1, r, dy, ga
 
         def stage2_p(i, copy):
             codes, scales = uq[i]
-            bank = psum.tile([P, 4, P], F32, name="d_bank", tag="h", bufs=2)
+            bank = psum.tile([P, 4, P], F32, name="d_bank", tag="h", bufs=3)
             for t in range(4):
                 for g in range(G):
                     nc.tensor.matmul_mx(
@@ -301,22 +309,21 @@ def tile_convnextdroppathlayerscaleweightgrad_x1_kernel(tc, x, w1, b1, r, dy, ga
         nc.scalar.activation(out=warm[:], in_=warm[:], func=GELU)
         vcopy(out=ident_bf[:], in_=ident[:])
         x00 = x_transpose(0, 0)
-        x01 = x_transpose(0, 1)
         c_bank = psum.tile([P, P], BF16, name="c_bank", tag="r", bufs=2)
         nc.tensor.transpose(c_bank[:], rows[:], ident_bf[:])
-        w_group(vcopy, 0, 1)
+        x01 = x_transpose(0, 1)
+        w_group(vcopy, 0, 2)
         x_exit(vcopy, 0, 0, x00)
-        x_exit(scopy, 0, 1, x01)
-        scopy(out=cols[:], in_=c_bank[:, 0:20])
         scopy(out=gcols[:], in_=c_bank[:, 16:20])
-        w_group(scopy, 1, 1)
+        scopy(out=cols[:], in_=c_bank[:, 0:20])
+        x_exit(scopy, 0, 1, x01)
+        w_quant(0, 2)
         g_bank = psum.tile([P, C], BF16, name="g_bank", tag="r", bufs=2)
         for q in range(4):
             nc.tensor.transpose(g_bank[:, q * P : (q + 1) * P], gcols[:, q : q + 1].to_broadcast([P, P]), ident_bf[:])
         scopy(out=gam[:], in_=g_bank[:])
-        w_quant(0, 1)
         x_quant(0)
-        w_quant(1, 1)
+
         x10 = x_transpose(1, 0)
         x11 = x_transpose(1, 1)
         x_exit(scopy, 1, 0, x10)
@@ -324,10 +331,11 @@ def tile_convnextdroppathlayerscaleweightgrad_x1_kernel(tc, x, w1, b1, r, dy, ga
         stage1(0, 0)
         stage1(1, 0)
         w_group(vcopy, 2, 2)
+        e_mult(0, 0, 1)
         x_quant(1)
         stage1(0, 1)
         stage1(1, 1)
-        e_mult(0, 0, 4)
+        e_mult(0, 1, 4)
         w_quant(2, 2)
         w_group(scopy, 4, 2)
         e_quant(0)
@@ -339,6 +347,7 @@ def tile_convnextdroppathlayerscaleweightgrad_x1_kernel(tc, x, w1, b1, r, dy, ga
             ahead = [i for i in (2 * k - 5, 2 * k - 4) if i >= 0]
             pair = k - 3
             paired = 0 <= 2 * pair < DIRECT
+            late = pair >= 9
             for n in range(2):
                 if lead < TILES:
                     stage1(lead, n)
@@ -350,38 +359,49 @@ def tile_convnextdroppathlayerscaleweightgrad_x1_kernel(tc, x, w1, b1, r, dy, ga
                 w_group(scopy, 6, 2)
             if lead < TILES:
                 stage1(lead + 1, 0)
-            if paired:
+            if paired and not late:
                 p_cast(pair)
             if even < TILES:
                 turn(even, 0)
                 turn(even, 1)
             if lead < TILES:
                 stage1(lead + 1, 1)
-            if paired:
+            if paired and not late:
                 p_turn(pair)
                 p_exit(pair, scopy)
+            if k in S_HALVES:
+                w_group(scopy, S_HALVES[k], 1)
             if even < TILES:
                 u_mult(even, 0)
                 u_mult(even, 1)
+            if paired and late:
+                p_cast(pair)
             if k == 1:
                 e_quant(1)
-            elif 2 * k + 4 < TILES:
-                w_quant(2 * k + 4, 2)
+            if k in QUANTS:
+                w_quant(QUANTS[k], 2)
             if even < TILES:
                 u_quant(even)
                 turn(odd, 0)
-            if even < TILES:
                 turn(odd, 1)
+            if paired and late:
+                p_turn(pair)
+                p_exit(pair, scopy)
+            if even < TILES:
                 u_mult(odd, 0)
                 u_mult(odd, 1)
             if k == 1:
                 w_quant(6, 2)
-            if 2 * k + 6 < TILES:
-                w_group(vcopy, 2 * k + 6, 2)
-            if paired:
+            if k in V_GROUPS:
+                w_group(vcopy, V_GROUPS[k], 2)
+            if paired and not late:
                 p_quant(pair)
+            if pair >= 1 and 2 * pair - 2 < DIRECT and pair - 1 >= 9 and even + 2 < TILES:
+                p_quant(pair - 1)
             if even < TILES:
                 u_quant(odd)
+            if pair >= 1 and 2 * pair - 2 < DIRECT and pair - 1 >= 9 and even + 2 >= TILES:
+                p_quant(pair - 1)
             for i in ahead:
                 if i >= DIRECT:
                     d_quant(i)

from contextlib import ExitStack

import concourse.mybir as mybir
from concourse.masks import make_identity

N, C, F = 1024, 512, 2048
FLOPS = 4 * N * C * F

F32 = mybir.dt.float32
BF16 = mybir.dt.bfloat16
I32 = mybir.dt.int32
U32 = mybir.dt.uint32
U8 = mybir.dt.uint8
FP8X4 = mybir.dt.float8_e4m3fn_x4
GELU = mybir.ActivationFunctionType.Gelu_apprx_tanh
MULT = mybir.AluOpType.mult

P = 128
G = N // 512
TILES = F // P
W_LOADS = ((0, 2), (2, 4), (4, 8), (8, 12), (12, 16))
S_HALVES = {2: 12, 3: 13}
V_GROUPS = {1: 8, 2: 10, 4: 14}
QUANTS = {2: 8, 3: 10, 4: 12, 5: 14}
DIRECT = 12


def tile_convnextdroppathlayerscaleweightgrad_x1_kernel(tc, x, w1, b1, r, dy, gamma, out_0, out_1, out_2):
    nc = tc.nc
    vcopy, scopy = nc.vector.tensor_copy, nc.scalar.copy
    with ExitStack() as ctx:
        keep = ctx.enter_context(tc.tile_pool(name="keep", bufs=1))
        work = ctx.enter_context(tc.tile_pool(name="work", bufs=3))
        psum = ctx.enter_context(tc.psum_pool(name="psum", bufs=1))
        ctx.enter_context(tc.manual_schedule())

        ident = keep.tile([P, P], F32, name="ident")
        ident_bf = keep.tile([P, P], BF16, name="ident_bf")
        rows = keep.tile([P, P], BF16, name="rows")
        cols = keep.tile([P, 20], F32, name="cols")
        gcols = keep.tile([P, 4], BF16, name="gcols")
        gam = keep.tile([P, C], BF16, name="gam")
        r_sb = keep.tile([P, G, 4], BF16, name="r_sb")
        warm = keep.tile([P, 1], F32, name="warm")
        x_raw = [keep.tile([P, 4, C], BF16, name=f"x_raw{g}") for g in range(G)]
        x_bf = [keep.tile([P, 4 * P, 4], BF16, name=f"x_bf{g}", align_bytes=64) for g in range(G)]
        x_codes = keep.tile([P, G, 512], U32, name="x_codes", align_bytes=64)
        x_scales = keep.tile([P, G, 512], U8, name="x_scales", align_bytes=64)
        w_raw = {}
        for i0, i1 in W_LOADS:
            raw = keep.tile([P, 4, (i1 - i0) * P], BF16, name=f"w_raw{i0}")
            for i in range(i0, i1):
                w_raw[i] = raw, i - i0
        w_codes = keep.tile([P, F], U32, name="w_codes", align_bytes=64)
        w_scales = keep.tile([P, F], U8, name="w_scales", align_bytes=64)
        dy_raw = [keep.tile([P, 4, C], BF16, name=f"dy_raw{g}") for g in range(G)]
        e_bf = [keep.tile([P, C, 4], BF16, name=f"e_bf{g}", align_bytes=64) for g in range(G)]
        e_codes = keep.tile([P, G, C], U32, name="e_codes", align_bytes=64)
        e_scales = keep.tile([P, G, C], U8, name="e_scales", align_bytes=64)
        p_codes = keep.tile([P, F], U32, name="p_codes", align_bytes=64)
        p_scales = keep.tile([P, F], U8, name="p_scales", align_bytes=64)

        def load_x(g, t0, t1):
            src = x[512 * g : 512 * g + 512, :].rearrange("(m t) k -> m t k", t=4)
            nc.sync.dma_start(out=x_raw[g][:, t0:t1, :], in_=src[:, t0:t1, :])

        def load_w(i0, i1):
            c = slice(i0 * P, i1 * P)
            nc.sync.dma_start(out=w_raw[i0][0][:], in_=w1[:, c].rearrange("(p j) f -> p j f", j=4))

        def load_dy(g):
            src = dy[512 * g : 512 * g + 512, :].rearrange("(p j) c -> p j c", j=4)
            nc.sync.dma_start(out=dy_raw[g][:], in_=src)

        def x_transpose(g, half):
            words = x_raw[g][:].rearrange("p t k -> p (t k)").bitcast(F32)
            bank = psum.tile([P, 2, 2, P], F32, name="x_bank", tag="t", bufs=3)
            for n in range(2):
                t = 2 * half + n
                for u in range(2):
                    nc.tensor.transpose(bank[:, n, u, :], words[:, 256 * t + u : 256 * (t + 1) : 2], ident[:])
            return bank

        def x_exit(copy, g, half, bank):
            dst = x_bf[g][:, 256 * half : 256 * half + 256, :].rearrange("p c j -> p (c j)").bitcast(F32)
            copy(
                out=dst.rearrange("p (t m u) -> p t m u", t=2, u=2),
                in_=bank[:].rearrange("p t u m -> p t m u"),
            )

        def x_quant(g):
            nc.vector.quantize_mx(
                out=x_codes[:, g, :].bitcast(FP8X4),
                scales=x_scales[:, g, :],
                in_=x_bf[g][:].rearrange("p c j -> p (c j)"),
            )

        wg = {}

        def w_group(copy, i, n):
            raw, at = w_raw[i]
            first = i - i % 2
            if i == first:
                wg[i] = work.tile([P, 2 * P, 4], BF16, name="w_bf", bufs=5, align_bytes=64)
            src = raw[:, :, at * P : (at + n) * P]
            dst = wg[first][:, (i - first) * P : (i - first + n) * P, :]
            copy(
                out=dst.rearrange("p (c q) j -> p c j q", q=4),
                in_=src.rearrange("p j (c q) -> p c j q", q=4),
            )

        def w_quant(i, n):
            c = slice(i * P, (i + n) * P)
            nc.vector.quantize_mx(
                out=w_codes[:, c].bitcast(FP8X4),
                scales=w_scales[:, c],
                in_=wg[i][:, : n * P, :].rearrange("p c j -> p (c j)"),
            )

        def e_mult(g, t0, t1):
            nc.vector.tensor_tensor(
                out=e_bf[g][:, t0 * P : t1 * P, :].rearrange("p (t m) j -> p t m j", m=P),
                in0=dy_raw[g][:].rearrange("p j (m t) -> p t m j", t=4)[:, t0:t1],
                in1=gam[:].rearrange("p (m t) -> p t m", t=4)[:, t0:t1].unsqueeze(3).to_broadcast([P, t1 - t0, P, 4]),
                op=MULT,
            )

        def e_quant(g):
            nc.vector.quantize_mx(
                out=e_codes[:, g, :].bitcast(FP8X4),
                scales=e_scales[:, g, :],
                in_=e_bf[g][:].rearrange("p c j -> p (c j)"),
            )

        a = {}

        def stage1(i, g):
            bank = psum.tile([P, 512], F32, name="h_bank", tag="h", bufs=3)
            c = slice(i * P, (i + 1) * P)
            nc.tensor.matmul_mx(
                out=bank[:],
                lhsT=w_codes[:, c].bitcast(FP8X4),
                lhsT_scale=w_scales[:, c],
                rhs=x_codes[:, g, :].bitcast(FP8X4),
                rhs_scale=x_scales[:, g, :],
                start=True,
                stop=True,
            )
            a[i, g] = work.tile([P, 512], F32, name="a_sb", bufs=8)
            nc.scalar.activation(out=a[i, g][:], in_=bank[:], func=GELU, bias=cols[:, i : i + 1])

        turned = {}
        u = {}

        def turn(i, g):
            turned[i, g] = psum.tile([P, 4, P], F32, name="t_bank", tag="t", bufs=3)
            for t in range(4):
                nc.tensor.transpose(turned[i, g][:, t, :], a[i, g][:, t * P : (t + 1) * P], ident[:])

        def u_mult(i, g):
            if g == 0:
                u[i] = work.tile([P, G, P, 4], BF16, name="u_bf", bufs=4, align_bytes=64)
            nc.vector.tensor_tensor(
                out=u[i][:, g, :, :],
                in0=turned[i, g][:].rearrange("p t f -> p f t"),
                in1=r_sb[:, g, :].unsqueeze(1).to_broadcast([P, P, 4]),
                op=MULT,
            )

        uq = {}

        def u_quant(i):
            codes = work.tile([P, G, P], U32, name="u_codes", bufs=8, align_bytes=64)
            scales = work.tile([P, G, P], U8, name="u_scales", bufs=8, align_bytes=64)
            nc.vector.quantize_mx(
                out=codes[:].rearrange("p g f -> p (g f)").bitcast(FP8X4),
                scales=scales[:].rearrange("p g f -> p (g f)"),
                in_=u[i][:].rearrange("p g f t -> p (g f t)"),
            )
            uq[i] = codes, scales

        r_out = {}

        def stage2_r(i, copy):
            codes, scales = uq[i]
            bank = psum.tile([P, C], F32, name="r_bank", tag="r", bufs=2)
            for g in range(G):
                nc.tensor.matmul_mx(
                    out=bank[:],
                    lhsT=codes[:, g, :].bitcast(FP8X4),
                    lhsT_scale=scales[:, g, :],
                    rhs=e_codes[:, g, :].bitcast(FP8X4),
                    rhs_scale=e_scales[:, g, :],
                    start=(g == 0),
                    stop=(g == G - 1),
                )
            j, n = divmod(i, 2)
            if n == 0:
                r_out[j] = work.tile([P, 2, C], F32, name="r_out", bufs=4)
            dst = r_out[j][:, n, :]
            copy(
                out=dst.rearrange("p (m t) -> p m t", t=4),
                in_=bank[:].rearrange("p (t m) -> p m t", t=4),
            )
            nc.sync.dma_start(out=out_0[i * P : (i + 1) * P, :], in_=dst)

        r_bf = {}
        p_turned = {}
        p_bf = {}

        def p_cast(j):
            r_bf[j] = work.tile([P, 2, 2, P, 2], BF16, name="r_bf", bufs=2)
            vcopy(
                out=r_bf[j][:].rearrange("p v n m c -> p v (n m) c"),
                in_=r_out[j][:].rearrange("p n (m v c) -> p v (n m) c", v=2, c=2),
            )

        def p_turn(j):
            words = r_bf[j][:].rearrange("p v n m c -> p (v n m c)").bitcast(F32)
            p_turned[j] = psum.tile([P, 2, 2, P], F32, name="p_bank", tag="r", bufs=2)
            for n in range(2):
                for v in range(2):
                    nc.tensor.transpose(p_turned[j][:, n, v, :], words[:, 128 * (2 * v + n) : 128 * (2 * v + n + 1)], ident[:])

        def p_exit(j, copy):
            p_bf[j] = work.tile([P, 2, P, 4], BF16, name="p_bf", bufs=3, align_bytes=64)
            dst = p_bf[j][:].rearrange("p n f c -> p (n f c)").bitcast(F32)
            copy(
                out=dst.rearrange("p (n f v) -> p n f v", n=2, v=2),
                in_=p_turned[j][:].rearrange("p n v f -> p n f v"),
            )

        def store_words(i0, i1):
            nc.sync.dma_start(
                out=out_1[0, :, i0 * P : i1 * P, :].rearrange("p m t -> p (m t)").bitcast(I32),
                in_=p_codes[:, i0 * P : i1 * P].bitcast(I32),
            )

        def store_scales(i0, i1):
            for quadrant in range(4):
                queue = nc.scalar if i1 == TILES and quadrant % 2 else nc.sync
                queue.dma_start(
                    out=out_2[0, 4 * quadrant : 4 * quadrant + 4, i0 * P : i1 * P].bitcast(I32),
                    in_=p_scales[32 * quadrant : 32 * quadrant + 4, i0 * P : i1 * P].bitcast(I32),
                )

        def p_quant(j):
            c = slice(2 * j * P, (2 * j + 2) * P)
            nc.vector.quantize_mx(
                out=p_codes[:, c].bitcast(FP8X4),
                scales=p_scales[:, c],
                in_=p_bf[j][:].rearrange("p n f c -> p (n f c)"),
            )
            if j % 2 == 1:
                store_words(2 * j - 2, 2 * j + 2)
            elif 2 * j + 2 == DIRECT:
                store_words(2 * j, 2 * j + 2)
            if 2 * j + 2 == DIRECT:
                store_scales(0, DIRECT)

        d_bf = {}

        def stage2_p(i, copy):
            codes, scales = uq[i]
            bank = psum.tile([P, 4, P], F32, name="d_bank", tag="h", bufs=3)
            for t in range(4):
                for g in range(G):
                    nc.tensor.matmul_mx(
                        out=bank[:, t, :],
                        lhsT=e_codes[:, g, t * P : (t + 1) * P].bitcast(FP8X4),
                        lhsT_scale=e_scales[:, g, t * P : (t + 1) * P],
                        rhs=codes[:, g, :].bitcast(FP8X4),
                        rhs_scale=scales[:, g, :],
                        start=(g == 0),
                        stop=(g == G - 1),
                    )
            d_bf[i] = work.tile([P, P, 4], BF16, name="d_bf", bufs=4, align_bytes=64)
            copy(out=d_bf[i][:], in_=bank[:].rearrange("p t f -> p f t"))

        def d_quant(i):
            c = slice(i * P, (i + 1) * P)
            nc.vector.quantize_mx(
                out=p_codes[:, c].bitcast(FP8X4),
                scales=p_scales[:, c],
                in_=d_bf[i][:].rearrange("p f t -> p (f t)"),
            )
            if i % 2 == 1:
                store_words(i - 1, i + 1)
            if i == TILES - 1:
                store_scales(DIRECT, TILES)

        nc.gpsimd.memset(rows[:], 0.0)
        nc.gpsimd.memset(warm[:], 0.0)
        make_identity(nc, ident[:])
        nc.scalar.dma_start(out=rows[0:16, :], in_=b1.rearrange("(i f) -> i f", f=P))
        nc.scalar.dma_start(out=rows[16:20, :], in_=gamma.rearrange("(i f) -> i f", f=P))
        nc.scalar.dma_start(out=r_sb[:], in_=r.rearrange("(g p t) -> p g t", g=G, t=4))
        load_x(0, 0, 2)
        load_x(0, 2, 4)
        load_w(0, 2)
        load_x(1, 0, 4)
        load_w(2, 4)
        load_dy(0)
        load_dy(1)
        load_w(4, 8)
        load_w(8, 12)
        load_w(12, 16)

        nc.scalar.activation(out=warm[:], in_=warm[:], func=GELU)
        vcopy(out=ident_bf[:], in_=ident[:])
        x00 = x_transpose(0, 0)
        c_bank = psum.tile([P, P], BF16, name="c_bank", tag="r", bufs=2)
        nc.tensor.transpose(c_bank[:], rows[:], ident_bf[:])
        x01 = x_transpose(0, 1)
        w_group(vcopy, 0, 2)
        x_exit(vcopy, 0, 0, x00)
        scopy(out=gcols[:], in_=c_bank[:, 16:20])
        scopy(out=cols[:], in_=c_bank[:, 0:20])
        x_exit(scopy, 0, 1, x01)
        w_quant(0, 2)
        g_bank = psum.tile([P, C], BF16, name="g_bank", tag="r", bufs=2)
        for q in range(4):
            nc.tensor.transpose(g_bank[:, q * P : (q + 1) * P], gcols[:, q : q + 1].to_broadcast([P, P]), ident_bf[:])
        scopy(out=gam[:], in_=g_bank[:])
        x_quant(0)

        x10 = x_transpose(1, 0)
        x11 = x_transpose(1, 1)
        x_exit(scopy, 1, 0, x10)
        x_exit(scopy, 1, 1, x11)
        stage1(0, 0)
        stage1(1, 0)
        w_group(vcopy, 2, 2)
        e_mult(0, 0, 1)
        x_quant(1)
        stage1(0, 1)
        stage1(1, 1)
        e_mult(0, 1, 4)
        w_quant(2, 2)
        w_group(scopy, 4, 2)
        e_quant(0)
        e_mult(1, 0, 4)
        w_quant(4, 2)

        for k in range(1, TILES // 2 + 2):
            lead, even, odd = 2 * k, 2 * k - 2, 2 * k - 1
            ahead = [i for i in (2 * k - 5, 2 * k - 4) if i >= 0]
            pair = k - 3
            paired = 0 <= 2 * pair < DIRECT
            late = pair >= 9
            for n in range(2):
                if lead < TILES:
                    stage1(lead, n)
                for i in ahead[n : n + 1] if len(ahead) == 2 else ahead[n - 1 : n]:
                    if i >= DIRECT:
                        stage2_p(i, scopy)
                    stage2_r(i, scopy)
            if k == 1:
                w_group(scopy, 6, 2)
            if lead < TILES:
                stage1(lead + 1, 0)
            if paired and not late:
                p_cast(pair)
            if even < TILES:
                turn(even, 0)
                turn(even, 1)
            if lead < TILES:
                stage1(lead + 1, 1)
            if paired and not late:
                p_turn(pair)
                p_exit(pair, scopy)
            if k in S_HALVES:
                w_group(scopy, S_HALVES[k], 1)
            if even < TILES:
                u_mult(even, 0)
                u_mult(even, 1)
            if paired and late:
                p_cast(pair)
            if k == 1:
                e_quant(1)
            if k in QUANTS:
                w_quant(QUANTS[k], 2)
            if even < TILES:
                u_quant(even)
                turn(odd, 0)
                turn(odd, 1)
            if paired and late:
                p_turn(pair)
                p_exit(pair, scopy)
            if even < TILES:
                u_mult(odd, 0)
                u_mult(odd, 1)
            if k == 1:
                w_quant(6, 2)
            if k in V_GROUPS:
                w_group(vcopy, V_GROUPS[k], 2)
            if paired and not late:
                p_quant(pair)
            if pair >= 1 and 2 * pair - 2 < DIRECT and pair - 1 >= 9 and even + 2 < TILES:
                p_quant(pair - 1)
            if even < TILES:
                u_quant(odd)
            if pair >= 1 and 2 * pair - 2 < DIRECT and pair - 1 >= 9 and even + 2 >= TILES:
                p_quant(pair - 1)
            for i in ahead:
                if i >= DIRECT:
                    d_quant(i)
        i = TILES - 1
        stage2_p(i, scopy)
        stage2_r(i, vcopy)
        d_quant(i)
